import numpy as np
import ml_dtypes


def mxq(x, axis, fmt="e4m3"):
    dtype, down = {"e4m3": (ml_dtypes.float8_e4m3fn, 7), "e5m2": (ml_dtypes.float8_e5m2, 14)}[fmt]
    v = np.moveaxis(np.asarray(x, np.float32).astype(ml_dtypes.bfloat16).astype(np.float64), axis, -1)
    blocks = v.reshape(v.shape[:-1] + (-1, 32))
    amax = np.abs(blocks).max(-1, keepdims=True)
    byte = np.maximum(np.where(amax > 0, np.frexp(amax)[1] - 1 + 127, 0) - down, 1)
    scale = np.exp2(byte - 127.0)
    codes = (blocks / scale).astype(np.float32).astype(dtype).astype(np.float64)
    return np.moveaxis((codes * scale).reshape(v.shape), -1, axis)


WIDE = False


def mx_kscale(k):
    if not WIDE:
        return np.ones(k)
    levels = np.array([10, -10, 5, -5, 0])
    if k % 512:
        return np.exp2(np.random.permutation(np.resize(levels, k // 32))).repeat(32)
    a = np.empty((k // 512, 16))
    for p in range(k // 512):
        a[p, :8] = np.random.permutation(np.resize(levels, 8))
        for g in range(8):
            far = levels[np.abs(levels - a[p, g]) >= 10]
            a[p, g + 8] = far[np.random.randint(len(far))]
    return np.exp2(a.ravel()).repeat(32)


def f64(x):
    return np.asarray(x).astype(np.float64)


def striped(idx):
    return np.tile(idx.reshape(-1, 16).T, (8, 1)).astype(np.uint16)


def unstriped(offs):
    return offs[:16].T.reshape(-1).astype(np.int64)


def striped8(idx):
    return np.concatenate([x.reshape(-1, 16).T for x in idx]).astype(np.uint16)


def runs(offs, k):
    lists = np.stack([offs[16 * r : 16 * r + 16].T.reshape(-1) for r in range(8)]).astype(np.int64)
    return lists[np.arange(k) % 512 // 64]


def pack_weight(w):
    k, n = w.shape
    w = f64(np.asarray(w, np.float32).astype(ml_dtypes.bfloat16)).reshape(k // 32, 32, n)
    amax = np.abs(w).max(1)
    byte = np.clip(np.where(amax > 0, np.frexp(amax)[1] - 1 + 127 - 7, 1), 1, 254)
    scaled = (w * np.exp2(127.0 - byte)[:, None, :]).reshape(k, n).astype(np.float32)
    words = np.ascontiguousarray(scaled.reshape(k // 512, 128, 4, n).transpose(0, 1, 3, 2)).astype(ml_dtypes.float8_e4m3fn).view(np.uint8)
    return words, np.ascontiguousarray(byte.astype(np.uint8).reshape(k // 512, 16, n))


def unpack_weight(words, scales):
    g, p, n, _ = words.shape
    vals = np.ascontiguousarray(words).view(ml_dtypes.float8_e4m3fn).astype(np.float64) * np.repeat(np.exp2(scales.astype(np.float64) - 127.0), 8, axis=1)[..., None]
    return vals.transpose(0, 1, 3, 2).reshape(g * 512, n)


K, T, S, H, G, U = 512, 2048, 256, 512, 2048, 512


def setup_inputs():
    n = np.random.standard_normal
    s = mx_kscale(K)[:, None]
    packed_xT = pack_weight(n((K, T)) * s)
    packed_dT = pack_weight(n((K, G)) / s)
    perm = np.random.permutation(U)
    return {
        "x_words": packed_xT[0],
        "x_scales": packed_xT[1],
        "w1": (n((K, H)) / np.sqrt(K) / s).astype(np.float32),
        "gs": (np.random.uniform(0.5, 1.5, (K, 1)) * s).astype(np.float32),
        "d_words": packed_dT[0],
        "d_scales": packed_dT[1],
        "offs": striped8(np.random.randint(0, T, (8, S))),
        "ka": striped8(np.random.randint(0, G, (8, H))),
        "kb": striped8(np.random.randint(0, G, (8, H))),
        "n1": striped(perm[:S]),
        "n2": striped(perm[S:]),
        "n3": striped(np.random.permutation(S)),
    }


def reference(x_words, x_scales, w1, gs, d_words, d_scales, offs, ka, kb, n1, n2, n3):
    d_ka = unpack_weight(d_words, d_scales)[np.arange(K)[:, None], runs(ka, K)]
    xq = unpack_weight(x_words, x_scales)[np.arange(K)[:, None], runs(offs, K)]
    y = mxq(f64(w1), 0, "e4m3").T @ xq
    z = f64(gs) * y
    zq = mxq(z, 0, "e4m3")
    d_kb = unpack_weight(d_words, d_scales)[np.arange(K)[:, None], runs(kb, K)]
    h = 0.0625 * (d_ka.T @ zq + d_kb.T @ zq)
    nw = h - h[:, unstriped(n3)]
    ph = np.zeros((H, U))
    ph[:, unstriped(n1)] = h
    out = ph.copy()
    out[:, unstriped(n2)] = nw
    return out

@@ -1,0 +1,162 @@
+from contextlib import ExitStack
+
+import concourse.mybir as mybir
+
+K, T, S, H, G, U = 512, 2048, 256, 512, 2048, 512
+FLOPS = 2 * K * H * S + 2 * 2 * K * H * S
+
+F32 = mybir.dt.float32
+BF16 = mybir.dt.bfloat16
+I32 = mybir.dt.int32
+U32 = mybir.dt.uint32
+U16 = mybir.dt.uint16
+U8 = mybir.dt.uint8
+FP8X4 = mybir.dt.float8_e4m3fn_x4
+COPY = mybir.ActivationFunctionType.Copy
+MULT = mybir.AluOpType.mult
+SUBTRACT = mybir.AluOpType.subtract
+
+P = 128
+PACK = 4
+STRIPE = 16
+PICK = 256
+HALF = S // 2
+SCALAR_SHARE = 64
+
+
+def entries(offsets, start, count):
+    return offsets[:, start // STRIPE : (start + count) // STRIPE]
+
+
+def tile_picked_hdaqipagq_none_p_kernel(
+    tc, x_words, x_scales, w1, gs, d_words, d_scales, offs, ka, kb, n1, n2, n3, out
+):
+    nc = tc.nc
+    with ExitStack() as ctx:
+        keep = ctx.enter_context(tc.tile_pool(name="keep", bufs=1))
+        psum = ctx.enter_context(tc.psum_pool(name="psum", bufs=1))
+
+        def load_list(name, source):
+            offsets = keep.tile(list(source.shape), U16, name=name)
+            nc.sync.dma_start(offsets[:], source)
+            return offsets
+
+        def load_scale_table(name, source):
+            table = keep.tile([P, source.shape[2]], U8, name=name, align_bytes=64)
+            nc.vector.memset(table[:].bitcast(I32), 0)
+            nc.scalar.dma_start(table[0:P:8, :].bitcast(I32), source[0].bitcast(I32))
+            return table
+
+        def load_word_table(name, source):
+            table = keep.tile([P, source.shape[2]], U32, name=name, align_bytes=64)
+            nc.sync.dma_start(table[:].bitcast(I32), source[0].rearrange("p n t -> p (n t)").bitcast(I32))
+            return table
+
+        def settle_scales(name, picked, width, queue):
+            plane = keep.tile([P, width], U8, name=name, align_bytes=64)
+            nc.vector.tensor_copy(plane[:].bitcast(I32), picked[:].bitcast(I32))
+            for r in range(1, 4):
+                queue.dma_start(plane[r:P:32, :].bitcast(I32), picked[8 * r : P : 32, :].bitcast(I32))
+            return plane
+
+        x_scale_table = load_scale_table("x_scale_table", x_scales)
+        d_scale_table = load_scale_table("d_scale_table", d_scales)
+        offs_sb = load_list("offs_sb", offs)
+        ka_sb = load_list("ka_sb", ka)
+        kb_sb = load_list("kb_sb", kb)
+        n3_sb = load_list("n3_sb", n3)
+        n1_sb = load_list("n1_sb", n1)
+        gs_sb = keep.tile([P, PACK], F32, name="gs_sb")
+        nc.gpsimd.dma_start(gs_sb[:], gs.rearrange("(p t) o -> p (t o)", t=PACK))
+        w_raw = keep.tile([P, PACK, H], F32, name="w_raw")
+        nc.sync.dma_start(w_raw[:], w1.rearrange("(p j) c -> p j c", j=PACK))
+        x_word_table = load_word_table("x_word_table", x_words)
+        d_word_table = load_word_table("d_word_table", d_words)
+        n2_sb = load_list("n2_sb", n2)
+
+        picked_first = keep.tile([P, S + 2 * PICK], U8, name="picked_first", align_bytes=64)
+        nc.vector.tensor_copy(picked_first[:, 0:S], x_scale_table[:].indirect(offs_sb[:]))
+        nc.vector.tensor_copy(picked_first[:, S : S + PICK], d_scale_table[:].indirect(entries(ka_sb, 0, PICK)))
+        nc.vector.tensor_copy(picked_first[:, S + PICK :], d_scale_table[:].indirect(entries(kb_sb, 0, PICK)))
+        plane_first = settle_scales("plane_first", picked_first, S + 2 * PICK, nc.scalar)
+
+        w_bf = keep.tile([P, PACK, P * PACK], BF16, name="w_bf", align_bytes=64)
+        w_out = w_bf[:].rearrange("p t (m j) -> p m j t", j=PACK)
+        w_in = w_raw[:].rearrange("p j (m t) -> p m j t", t=PACK)
+        nc.scalar.activation(w_out[:, 0:SCALAR_SHARE], w_in[:, 0:SCALAR_SHARE], COPY)
+        nc.vector.tensor_copy(w_out[:, SCALAR_SHARE:], w_in[:, SCALAR_SHARE:])
+        w_codes = keep.tile([P, H], U32, name="w_codes", align_bytes=64)
+        w_plane = keep.tile([P, H], U8, name="w_plane", align_bytes=64)
+        nc.vector.quantize_mx(w_codes[:].bitcast(FP8X4), w_plane[:], w_bf[:].rearrange("p t c -> p (t c)"))
+
+        x_codes = keep.tile([P, S], U32, name="x_codes", align_bytes=64)
+        nc.vector.tensor_copy(x_codes[:], x_word_table[:].indirect(offs_sb[:]))
+
+        z_bf = keep.tile([P, S, PACK], BF16, name="z_bf", tag="late", align_bytes=64)
+        for half in range(2):
+            cols = slice(half * HALF, (half + 1) * HALF)
+            y = psum.tile([P, PACK, HALF], F32, name="y%d" % half)
+            for t in range(PACK):
+                rows = slice(t * P, (t + 1) * P)
+                nc.tensor.matmul_mx(
+                    y[:, t, :],
+                    lhsT=w_codes[:, rows].bitcast(FP8X4),
+                    lhsT_scale=w_plane[:, rows],
+                    rhs=x_codes[:, cols].bitcast(FP8X4),
+                    rhs_scale=plane_first[:, cols],
+                    start=True,
+                    stop=True,
+                )
+            nc.vector.tensor_tensor(
+                z_bf[:, cols, :],
+                y[:].rearrange("p t j -> p j t"),
+                gs_sb[:].unsqueeze(1).to_broadcast([P, HALF, PACK]),
+                MULT,
+            )
+        z_codes = keep.tile([P, S], U32, name="z_codes", align_bytes=64)
+        z_plane = keep.tile([P, S], U8, name="z_plane", align_bytes=64)
+        nc.vector.quantize_mx(z_codes[:].bitcast(FP8X4), z_plane[:], z_bf[:].rearrange("p j t -> p (j t)"))
+
+        for part in range(H // PICK):
+            if part == 0:
+                plane, first = plane_first, S
+            else:
+                picked_late = keep.tile([P, 2 * PICK], U8, name="picked_late", tag="late", align_bytes=64)
+                nc.vector.tensor_copy(picked_late[:, 0:PICK], d_scale_table[:].indirect(entries(ka_sb, PICK, PICK)))
+                nc.vector.tensor_copy(picked_late[:, PICK:], d_scale_table[:].indirect(entries(kb_sb, PICK, PICK)))
+                plane, first = settle_scales("plane_late", picked_late, 2 * PICK, nc.sync), 0
+            codes = []
+            for name, offsets in (("a", ka_sb), ("b", kb_sb)):
+                picked_words = keep.tile([P, PICK], U32, name="d_codes_%s%d" % (name, part), tag="d_codes_" + name, align_bytes=64)
+                nc.vector.tensor_copy(picked_words[:], d_word_table[:].indirect(entries(offsets, part * PICK, PICK)))
+                codes.append(picked_words)
+            for block in range(PICK // P):
+                a = part * (PICK // P) + block
+                acc = psum.tile([P, S], F32, name="acc%d" % a)
+                for side in range(2):
+                    at = first + side * PICK + block * P
+                    nc.tensor.matmul_mx(
+                        acc[:],
+                        lhsT=codes[side][:, block * P : (block + 1) * P].bitcast(FP8X4),
+                        lhsT_scale=plane[:, at : at + P],
+                        rhs=z_codes[:].bitcast(FP8X4),
+                        rhs_scale=z_plane[:],
+                        start=(side == 0),
+                        stop=(side == 1),
+                    )
+                h = keep.tile([P, S], F32, name="h%d" % a)
+                if a == 0:
+                    nc.scalar.activation(h[:], acc[:], COPY, scale=0.0625)
+                else:
+                    nc.vector.tensor_scalar(h[:], acc[:], 0.0625, None, MULT)
+                fetched = keep.tile([P, S], F32, name="fetched%d" % a)
+                for half in range(2):
+                    nc.scalar.activation(
+                        fetched[:, half * HALF : (half + 1) * HALF], h[:].indirect(entries(n3_sb, half * HALF, HALF)), COPY
+                    )
+                nw = keep.tile([P, S], F32, name="nw%d" % a)
+                nc.vector.tensor_tensor(nw[:], h[:], fetched[:], SUBTRACT)
+                page = keep.tile([P, U], F32, name="page%d" % a)
+                nc.scalar.activation(page[:].indirect(n1_sb[:]), h[:], COPY)
+                nc.scalar.activation(page[:].indirect(n2_sb[:]), nw[:], COPY)
+                nc.sync.dma_start(out[a * P : (a + 1) * P, :], page[:])

@@ -21,7 +21,8 @@ PACK = 4
 STRIPE = 16
 PICK = 256
 HALF = S // 2
-SCALAR_SHARE = 64
+SCALAR_SHARE = 56
+SPARE = 16
 
 
 def entries(offsets, start, count):
@@ -41,44 +42,45 @@ def tile_picked_hdaqipagq_none_p_kernel(
             nc.sync.dma_start(offsets[:], source)
             return offsets
 
-        def load_scale_table(name, source):
+        def load_scale_table(name, source, zeroing_engine, queue):
             table = keep.tile([P, source.shape[2]], U8, name=name, align_bytes=64)
-            nc.vector.memset(table[:].bitcast(I32), 0)
-            nc.scalar.dma_start(table[0:P:8, :].bitcast(I32), source[0].bitcast(I32))
+            zeroing_engine.memset(table[:].bitcast(I32), 0)
+            queue.dma_start(table[0:P:8, :].bitcast(I32), source[0].bitcast(I32))
             return table
 
         def load_word_table(name, source):
-            table = keep.tile([P, source.shape[2]], U32, name=name, align_bytes=64)
+            table = keep.tile([P, source.shape[2]], U32, name=name, tag=name, align_bytes=64)
             nc.sync.dma_start(table[:].bitcast(I32), source[0].rearrange("p n t -> p (n t)").bitcast(I32))
             return table
 
-        def settle_scales(name, picked, width, queue):
+        def settle_scales(name, picked, width):
             plane = keep.tile([P, width], U8, name=name, align_bytes=64)
             nc.vector.tensor_copy(plane[:].bitcast(I32), picked[:].bitcast(I32))
             for r in range(1, 4):
-                queue.dma_start(plane[r:P:32, :].bitcast(I32), picked[8 * r : P : 32, :].bitcast(I32))
+                nc.sync.dma_start(plane[r:P:32, :].bitcast(I32), picked[8 * r : P : 32, :].bitcast(I32))
             return plane
 
-        x_scale_table = load_scale_table("x_scale_table", x_scales)
-        d_scale_table = load_scale_table("d_scale_table", d_scales)
+        gs_sb = keep.tile([P, PACK], F32, name="gs_sb")
+        nc.scalar.dma_start(gs_sb[:], gs.rearrange("(p t) o -> p (t o)", t=PACK))
         offs_sb = load_list("offs_sb", offs)
         ka_sb = load_list("ka_sb", ka)
-        kb_sb = load_list("kb_sb", kb)
-        n3_sb = load_list("n3_sb", n3)
-        n1_sb = load_list("n1_sb", n1)
-        gs_sb = keep.tile([P, PACK], F32, name="gs_sb")
-        nc.gpsimd.dma_start(gs_sb[:], gs.rearrange("(p t) o -> p (t o)", t=PACK))
+        x_scale_table = load_scale_table("x_scale_table", x_scales, nc.vector, nc.sync)
+        d_scale_table = load_scale_table("d_scale_table", d_scales, nc.gpsimd, nc.scalar)
         w_raw = keep.tile([P, PACK, H], F32, name="w_raw")
         nc.sync.dma_start(w_raw[:], w1.rearrange("(p j) c -> p j c", j=PACK))
         x_word_table = load_word_table("x_word_table", x_words)
-        d_word_table = load_word_table("d_word_table", d_words)
-        n2_sb = load_list("n2_sb", n2)
+        kb_sb = load_list("kb_sb", kb)
 
-        picked_first = keep.tile([P, S + 2 * PICK], U8, name="picked_first", align_bytes=64)
-        nc.vector.tensor_copy(picked_first[:, 0:S], x_scale_table[:].indirect(offs_sb[:]))
-        nc.vector.tensor_copy(picked_first[:, S : S + PICK], d_scale_table[:].indirect(entries(ka_sb, 0, PICK)))
-        nc.vector.tensor_copy(picked_first[:, S + PICK :], d_scale_table[:].indirect(entries(kb_sb, 0, PICK)))
-        plane_first = settle_scales("plane_first", picked_first, S + 2 * PICK, nc.scalar)
+        x_picked = keep.tile([P, S], U8, name="x_picked", align_bytes=64)
+        nc.vector.tensor_copy(x_picked[:], x_scale_table[:].indirect(offs_sb[:]))
+        x_plane = settle_scales("x_plane", x_picked, S)
+        d_word_table = load_word_table("d_word_table", d_words)
+        a_picked = keep.tile([P, H], U8, name="a_picked", align_bytes=64)
+        nc.vector.tensor_copy(a_picked[:], d_scale_table[:].indirect(ka_sb[:]))
+        a_plane = settle_scales("a_plane", a_picked, H)
+        n3_sb = load_list("n3_sb", n3)
+        n1_sb = load_list("n1_sb", n1)
+        n2_sb = load_list("n2_sb", n2)
 
         w_bf = keep.tile([P, PACK, P * PACK], BF16, name="w_bf", align_bytes=64)
         w_out = w_bf[:].rearrange("p t (m j) -> p m j t", j=PACK)
@@ -92,7 +94,12 @@ def tile_picked_hdaqipagq_none_p_kernel(
         x_codes = keep.tile([P, S], U32, name="x_codes", align_bytes=64)
         nc.vector.tensor_copy(x_codes[:], x_word_table[:].indirect(offs_sb[:]))
 
-        z_bf = keep.tile([P, S, PACK], BF16, name="z_bf", tag="late", align_bytes=64)
+        b_picked = keep.tile([P, H], U8, name="b_picked", tag="x_word_table", align_bytes=64)
+        nc.vector.tensor_copy(b_picked[:], d_scale_table[:].indirect(kb_sb[:]))
+        b_plane = settle_scales("b_plane", b_picked, H)
+        d_planes = (a_plane, b_plane)
+
+        z_bf = keep.tile([P, S, PACK], BF16, name="z_bf", align_bytes=64)
         for half in range(2):
             cols = slice(half * HALF, (half + 1) * HALF)
             y = psum.tile([P, PACK, HALF], F32, name="y%d" % half)
@@ -103,7 +110,7 @@ def tile_picked_hdaqipagq_none_p_kernel(
                     lhsT=w_codes[:, rows].bitcast(FP8X4),
                     lhsT_scale=w_plane[:, rows],
                     rhs=x_codes[:, cols].bitcast(FP8X4),
-                    rhs_scale=plane_first[:, cols],
+                    rhs_scale=x_plane[:, cols],
                     start=True,
                     stop=True,
                 )
@@ -115,48 +122,60 @@ def tile_picked_hdaqipagq_none_p_kernel(
             )
         z_codes = keep.tile([P, S], U32, name="z_codes", align_bytes=64)
         z_plane = keep.tile([P, S], U8, name="z_plane", align_bytes=64)
-        nc.vector.quantize_mx(z_codes[:].bitcast(FP8X4), z_plane[:], z_bf[:].rearrange("p j t -> p (j t)"))
+        for half in range(2):
+            cols = slice(half * HALF, (half + 1) * HALF)
+            nc.vector.quantize_mx(
+                z_codes[:, cols].bitcast(FP8X4), z_plane[:, cols], z_bf[:, cols, :].rearrange("p j t -> p (j t)")
+            )
 
-        for part in range(H // PICK):
-            if part == 0:
-                plane, first = plane_first, S
-            else:
-                picked_late = keep.tile([P, 2 * PICK], U8, name="picked_late", tag="late", align_bytes=64)
-                nc.vector.tensor_copy(picked_late[:, 0:PICK], d_scale_table[:].indirect(entries(ka_sb, PICK, PICK)))
-                nc.vector.tensor_copy(picked_late[:, PICK:], d_scale_table[:].indirect(entries(kb_sb, PICK, PICK)))
-                plane, first = settle_scales("plane_late", picked_late, 2 * PICK, nc.sync), 0
+        def pick_words(part):
             codes = []
             for name, offsets in (("a", ka_sb), ("b", kb_sb)):
-                picked_words = keep.tile([P, PICK], U32, name="d_codes_%s%d" % (name, part), tag="d_codes_" + name, align_bytes=64)
-                nc.vector.tensor_copy(picked_words[:], d_word_table[:].indirect(entries(offsets, part * PICK, PICK)))
-                codes.append(picked_words)
-            for block in range(PICK // P):
-                a = part * (PICK // P) + block
-                acc = psum.tile([P, S], F32, name="acc%d" % a)
-                for side in range(2):
-                    at = first + side * PICK + block * P
-                    nc.tensor.matmul_mx(
-                        acc[:],
-                        lhsT=codes[side][:, block * P : (block + 1) * P].bitcast(FP8X4),
-                        lhsT_scale=plane[:, at : at + P],
-                        rhs=z_codes[:].bitcast(FP8X4),
-                        rhs_scale=z_plane[:],
-                        start=(side == 0),
-                        stop=(side == 1),
-                    )
-                h = keep.tile([P, S], F32, name="h%d" % a)
-                if a == 0:
-                    nc.scalar.activation(h[:], acc[:], COPY, scale=0.0625)
-                else:
-                    nc.vector.tensor_scalar(h[:], acc[:], 0.0625, None, MULT)
-                fetched = keep.tile([P, S], F32, name="fetched%d" % a)
-                for half in range(2):
-                    nc.scalar.activation(
-                        fetched[:, half * HALF : (half + 1) * HALF], h[:].indirect(entries(n3_sb, half * HALF, HALF)), COPY
-                    )
-                nw = keep.tile([P, S], F32, name="nw%d" % a)
-                nc.vector.tensor_tensor(nw[:], h[:], fetched[:], SUBTRACT)
-                page = keep.tile([P, U], F32, name="page%d" % a)
-                nc.scalar.activation(page[:].indirect(n1_sb[:]), h[:], COPY)
-                nc.scalar.activation(page[:].indirect(n2_sb[:]), nw[:], COPY)
-                nc.sync.dma_start(out[a * P : (a + 1) * P, :], page[:])
+                picked = keep.tile([P, PICK], U32, name="d_codes_%s%d" % (name, part), tag="d_codes_" + name, align_bytes=64)
+                nc.vector.tensor_copy(picked[:], d_word_table[:].indirect(entries(offsets, part * PICK, PICK)))
+                codes.append(picked)
+            return codes
+
+        def make_h(a, codes):
+            block = a % (PICK // P)
+            acc = psum.tile([P, S], F32, name="acc%d" % a)
+            for side in range(2):
+                nc.tensor.matmul_mx(
+                    acc[:],
+                    lhsT=codes[side][:, block * P : (block + 1) * P].bitcast(FP8X4),
+                    lhsT_scale=d_planes[side][:, a * P : (a + 1) * P],
+                    rhs=z_codes[:].bitcast(FP8X4),
+                    rhs_scale=z_plane[:],
+                    start=(side == 0),
+                    stop=(side == 1),
+                )
+            h = keep.tile([P, S + SPARE], F32, name="h%d" % a)
+            nc.vector.memset(h[:, S:], 0.0)
+            if a == 0:
+                nc.scalar.activation(h[:, 0:S], acc[:], COPY, scale=0.0625)
+            else:
+                nc.vector.tensor_scalar(h[:, 0:S], acc[:], 0.0625, None, MULT)
+            return h
+
+        def place_h(a, h):
+            fetched = keep.tile([P, S], F32, name="fetched%d" % a)
+            nc.scalar.activation(fetched[:], h[:].indirect(n3_sb[:]), COPY)
+            nw = keep.tile([P, S], F32, name="nw%d" % a)
+            nc.vector.tensor_tensor(nw[:], h[:, 0:S], fetched[:], SUBTRACT)
+            page = keep.tile([P, U], F32, name="page%d" % a)
+            nc.scalar.activation(page[:].indirect(n1_sb[:]), h[:, 0:S], COPY)
+            return page, nw
+
+        def place_nw(a, page, nw):
+            nc.scalar.activation(page[:].indirect(n2_sb[:]), nw[:], COPY)
+            nc.sync.dma_start(out[a * P : (a + 1) * P, :], page[:])
+
+        waiting = None
+        for a in range(H // P):
+            if a % (PICK // P) == 0:
+                codes = pick_words(a // (PICK // P))
+            placed = place_h(a, make_h(a, codes))
+            if waiting is not None:
+                place_nw(a - 1, *waiting)
+            waiting = placed
+        place_nw(H // P - 1, *waiting)

@@ -21,7 +21,7 @@ PACK = 4
 STRIPE = 16
 PICK = 256
 HALF = S // 2
-SCALAR_SHARE = 56
+SCALAR_SHARE = 80
 SPARE = 16
 
 
@@ -55,8 +55,8 @@ def tile_picked_hdaqipagq_none_p_kernel(
 
         def settle_scales(name, picked, width):
             plane = keep.tile([P, width], U8, name=name, align_bytes=64)
-            nc.vector.tensor_copy(plane[:].bitcast(I32), picked[:].bitcast(I32))
-            for r in range(1, 4):
+            nc.vector.memset(plane[:].bitcast(I32), 0)
+            for r in range(4):
                 nc.sync.dma_start(plane[r:P:32, :].bitcast(I32), picked[8 * r : P : 32, :].bitcast(I32))
             return plane
 
@@ -65,9 +65,9 @@ def tile_picked_hdaqipagq_none_p_kernel(
         offs_sb = load_list("offs_sb", offs)
         ka_sb = load_list("ka_sb", ka)
         x_scale_table = load_scale_table("x_scale_table", x_scales, nc.vector, nc.sync)
-        d_scale_table = load_scale_table("d_scale_table", d_scales, nc.gpsimd, nc.scalar)
         w_raw = keep.tile([P, PACK, H], F32, name="w_raw")
         nc.sync.dma_start(w_raw[:], w1.rearrange("(p j) c -> p j c", j=PACK))
+        d_scale_table = load_scale_table("d_scale_table", d_scales, nc.vector, nc.sync)
         x_word_table = load_word_table("x_word_table", x_words)
         kb_sb = load_list("kb_sb", kb)
 
@@ -129,11 +129,9 @@ def tile_picked_hdaqipagq_none_p_kernel(
             )
 
         def pick_words(part):
-            codes = []
-            for name, offsets in (("a", ka_sb), ("b", kb_sb)):
-                picked = keep.tile([P, PICK], U32, name="d_codes_%s%d" % (name, part), tag="d_codes_" + name, align_bytes=64)
-                nc.vector.tensor_copy(picked[:], d_word_table[:].indirect(entries(offsets, part * PICK, PICK)))
-                codes.append(picked)
+            codes = keep.tile([P, 2 * PICK], U32, name="d_codes%d" % part, tag="d_codes", align_bytes=64)
+            for side, offsets in enumerate((ka_sb, kb_sb)):
+                nc.vector.tensor_copy(codes[:, side * PICK : (side + 1) * PICK], d_word_table[:].indirect(entries(offsets, part * PICK, PICK)))
             return codes
 
         def make_h(a, codes):
@@ -142,7 +140,7 @@ def tile_picked_hdaqipagq_none_p_kernel(
             for side in range(2):
                 nc.tensor.matmul_mx(
                     acc[:],
-                    lhsT=codes[side][:, block * P : (block + 1) * P].bitcast(FP8X4),
+                    lhsT=codes[:, side * PICK + block * P : side * PICK + (block + 1) * P].bitcast(FP8X4),
                     lhsT_scale=d_planes[side][:, a * P : (a + 1) * P],
                     rhs=z_codes[:].bitcast(FP8X4),
                     rhs_scale=z_plane[:],

@@ -21,8 +21,9 @@ PACK = 4
 STRIPE = 16
 PICK = 256
 HALF = S // 2
-SCALAR_SHARE = 80
+SCALAR_SHARE = 64
 SPARE = 16
+EARLY_ROWS = 2
 
 
 def entries(offsets, start, count):
@@ -49,35 +50,41 @@ def tile_picked_hdaqipagq_none_p_kernel(
             return table
 
         def load_word_table(name, source):
-            table = keep.tile([P, source.shape[2]], U32, name=name, tag=name, align_bytes=64)
+            table = keep.tile([P, source.shape[2]], U32, name=name, align_bytes=64)
             nc.sync.dma_start(table[:].bitcast(I32), source[0].rearrange("p n t -> p (n t)").bitcast(I32))
             return table
 
-        def settle_scales(name, picked, width):
+        def settle_scales(name, picked, width, queues):
             plane = keep.tile([P, width], U8, name=name, align_bytes=64)
             nc.vector.memset(plane[:].bitcast(I32), 0)
             for r in range(4):
-                nc.sync.dma_start(plane[r:P:32, :].bitcast(I32), picked[8 * r : P : 32, :].bitcast(I32))
+                queues[r % len(queues)].dma_start(plane[r:P:32, :].bitcast(I32), picked[8 * r : P : 32, :].bitcast(I32))
             return plane
 
         gs_sb = keep.tile([P, PACK], F32, name="gs_sb")
         nc.scalar.dma_start(gs_sb[:], gs.rearrange("(p t) o -> p (t o)", t=PACK))
-        offs_sb = load_list("offs_sb", offs)
-        ka_sb = load_list("ka_sb", ka)
-        x_scale_table = load_scale_table("x_scale_table", x_scales, nc.vector, nc.sync)
         w_raw = keep.tile([P, PACK, H], F32, name="w_raw")
-        nc.sync.dma_start(w_raw[:], w1.rearrange("(p j) c -> p j c", j=PACK))
+        w_rows = w1.rearrange("(p j) c -> p j c", j=PACK)
+        nc.sync.dma_start(w_raw[:, 0:EARLY_ROWS, :], w_rows[:, 0:EARLY_ROWS, :])
+        offs_sb = load_list("offs_sb", offs)
+        x_scale_table = load_scale_table("x_scale_table", x_scales, nc.vector, nc.sync)
+        ka_sb = load_list("ka_sb", ka)
         d_scale_table = load_scale_table("d_scale_table", d_scales, nc.vector, nc.sync)
+        nc.sync.dma_start(w_raw[:, EARLY_ROWS:, :], w_rows[:, EARLY_ROWS:, :])
         x_word_table = load_word_table("x_word_table", x_words)
         kb_sb = load_list("kb_sb", kb)
 
+        h_blocks = [keep.tile([P, S + SPARE], F32, name="h%d" % a) for a in range(H // P)]
+        nc.vector.memset(h_blocks[0][:, S:], 0.0)
+        for h in h_blocks[1:]:
+            nc.scalar.activation(h[:, S:], h_blocks[0][:, S:], COPY)
+
         x_picked = keep.tile([P, S], U8, name="x_picked", align_bytes=64)
         nc.vector.tensor_copy(x_picked[:], x_scale_table[:].indirect(offs_sb[:]))
-        x_plane = settle_scales("x_plane", x_picked, S)
+        x_plane = settle_scales("x_plane", x_picked, S, (nc.sync,))
         d_word_table = load_word_table("d_word_table", d_words)
-        a_picked = keep.tile([P, H], U8, name="a_picked", align_bytes=64)
-        nc.vector.tensor_copy(a_picked[:], d_scale_table[:].indirect(ka_sb[:]))
-        a_plane = settle_scales("a_plane", a_picked, H)
+        d_picked = keep.tile([P, 2 * H], U8, name="d_picked", align_bytes=64)
+        nc.vector.tensor_copy(d_picked[:, 0:H], d_scale_table[:].indirect(ka_sb[:]))
         n3_sb = load_list("n3_sb", n3)
         n1_sb = load_list("n1_sb", n1)
         n2_sb = load_list("n2_sb", n2)
@@ -94,10 +101,8 @@ def tile_picked_hdaqipagq_none_p_kernel(
         x_codes = keep.tile([P, S], U32, name="x_codes", align_bytes=64)
         nc.vector.tensor_copy(x_codes[:], x_word_table[:].indirect(offs_sb[:]))
 
-        b_picked = keep.tile([P, H], U8, name="b_picked", tag="x_word_table", align_bytes=64)
-        nc.vector.tensor_copy(b_picked[:], d_scale_table[:].indirect(kb_sb[:]))
-        b_plane = settle_scales("b_plane", b_picked, H)
-        d_planes = (a_plane, b_plane)
+        nc.vector.tensor_copy(d_picked[:, H:], d_scale_table[:].indirect(kb_sb[:]))
+        d_plane = settle_scales("d_plane", d_picked, 2 * H, (nc.sync, nc.scalar))
 
         z_bf = keep.tile([P, S, PACK], BF16, name="z_bf", align_bytes=64)
         for half in range(2):
@@ -141,18 +146,14 @@ def tile_picked_hdaqipagq_none_p_kernel(
                 nc.tensor.matmul_mx(
                     acc[:],
                     lhsT=codes[:, side * PICK + block * P : side * PICK + (block + 1) * P].bitcast(FP8X4),
-                    lhsT_scale=d_planes[side][:, a * P : (a + 1) * P],
+                    lhsT_scale=d_plane[:, side * H + a * P : side * H + (a + 1) * P],
                     rhs=z_codes[:].bitcast(FP8X4),
                     rhs_scale=z_plane[:],
                     start=(side == 0),
                     stop=(side == 1),
                 )
-            h = keep.tile([P, S + SPARE], F32, name="h%d" % a)
-            nc.vector.memset(h[:, S:], 0.0)
-            if a == 0:
-                nc.scalar.activation(h[:, 0:S], acc[:], COPY, scale=0.0625)
-            else:
-                nc.vector.tensor_scalar(h[:, 0:S], acc[:], 0.0625, None, MULT)
+            h = h_blocks[a]
+            nc.vector.tensor_scalar(h[:, 0:S], acc[:], 0.0625, None, MULT)
             return h
 
         def place_h(a, h):

@@ -37,6 +37,7 @@ def tile_picked_hdaqipagq_none_p_kernel(
     with ExitStack() as ctx:
         keep = ctx.enter_context(tc.tile_pool(name="keep", bufs=1))
         psum = ctx.enter_context(tc.psum_pool(name="psum", bufs=1))
+        accs = ctx.enter_context(tc.psum_pool(name="accs", bufs=6))
 
         def load_list(name, source):
             offsets = keep.tile(list(source.shape), U16, name=name)
@@ -83,7 +84,7 @@ def tile_picked_hdaqipagq_none_p_kernel(
         nc.vector.tensor_copy(x_picked[:], x_scale_table[:].indirect(offs_sb[:]))
         x_plane = settle_scales("x_plane", x_picked, S, (nc.sync,))
         d_word_table = load_word_table("d_word_table", d_words)
-        d_picked = keep.tile([P, 2 * H], U8, name="d_picked", align_bytes=64)
+        d_picked = keep.tile([P, 2 * H], U8, name="d_picked", tag="d_picked", align_bytes=64)
         nc.vector.tensor_copy(d_picked[:, 0:H], d_scale_table[:].indirect(ka_sb[:]))
         n3_sb = load_list("n3_sb", n3)
         n1_sb = load_list("n1_sb", n1)
@@ -104,8 +105,7 @@ def tile_picked_hdaqipagq_none_p_kernel(
         nc.vector.tensor_copy(d_picked[:, H:], d_scale_table[:].indirect(kb_sb[:]))
         d_plane = settle_scales("d_plane", d_picked, 2 * H, (nc.sync, nc.scalar))
 
-        z_bf = keep.tile([P, S, PACK], BF16, name="z_bf", align_bytes=64)
-        for half in range(2):
+        def project(half):
             cols = slice(half * HALF, (half + 1) * HALF)
             y = psum.tile([P, PACK, HALF], F32, name="y%d" % half)
             for t in range(PACK):
@@ -119,19 +119,31 @@ def tile_picked_hdaqipagq_none_p_kernel(
                     start=True,
                     stop=True,
                 )
-            nc.vector.tensor_tensor(
-                z_bf[:, cols, :],
-                y[:].rearrange("p t j -> p j t"),
-                gs_sb[:].unsqueeze(1).to_broadcast([P, HALF, PACK]),
-                MULT,
-            )
-        z_codes = keep.tile([P, S], U32, name="z_codes", align_bytes=64)
-        z_plane = keep.tile([P, S], U8, name="z_plane", align_bytes=64)
-        for half in range(2):
-            cols = slice(half * HALF, (half + 1) * HALF)
-            nc.vector.quantize_mx(
-                z_codes[:, cols].bitcast(FP8X4), z_plane[:, cols], z_bf[:, cols, :].rearrange("p j t -> p (j t)")
-            )
+            return y
+
+        def quantise_z(half, z_bf, tag):
+            codes = keep.tile([P, HALF], U32, name="z_codes%d" % half, tag=tag, align_bytes=64)
+            plane = keep.tile([P, HALF], U8, name="z_plane%d" % half, align_bytes=64)
+            nc.vector.quantize_mx(codes[:].bitcast(FP8X4), plane[:], z_bf[:].rearrange("p j t -> p (j t)"))
+            return codes, plane
+
+        y_first, y_second = project(0), project(1)
+        z_first = keep.tile([P, HALF, PACK], BF16, name="z_first", align_bytes=64)
+        nc.vector.tensor_tensor(
+            z_first[:],
+            y_first[:].rearrange("p t j -> p j t"),
+            gs_sb[:].unsqueeze(1).to_broadcast([P, HALF, PACK]),
+            MULT,
+        )
+        z_rows = keep.tile([P, PACK, HALF], BF16, name="z_rows", align_bytes=64)
+        for t in range(PACK):
+            nc.scalar.activation(z_rows[:, t, :], y_second[:, t, :], COPY, scale=gs_sb[:, t : t + 1])
+        z_second = keep.tile([P, HALF, PACK], BF16, name="z_second", align_bytes=64)
+        nc.scalar.copy(
+            z_second[:].rearrange("p (c i) t -> p c t i", i=PACK),
+            z_rows[:].rearrange("p t (c i) -> p c t i", i=PACK),
+        )
+        z_halves = (quantise_z(0, z_first, "z_codes0"), quantise_z(1, z_second, "d_picked"))
 
         def pick_words(part):
             codes = keep.tile([P, 2 * PICK], U32, name="d_codes%d" % part, tag="d_codes", align_bytes=64)
@@ -141,28 +153,31 @@ def tile_picked_hdaqipagq_none_p_kernel(
 
         def make_h(a, codes):
             block = a % (PICK // P)
-            acc = psum.tile([P, S], F32, name="acc%d" % a)
-            for side in range(2):
-                nc.tensor.matmul_mx(
-                    acc[:],
-                    lhsT=codes[:, side * PICK + block * P : side * PICK + (block + 1) * P].bitcast(FP8X4),
-                    lhsT_scale=d_plane[:, side * H + a * P : side * H + (a + 1) * P],
-                    rhs=z_codes[:].bitcast(FP8X4),
-                    rhs_scale=z_plane[:],
-                    start=(side == 0),
-                    stop=(side == 1),
-                )
-            h = h_blocks[a]
-            nc.vector.tensor_scalar(h[:, 0:S], acc[:], 0.0625, None, MULT)
-            return h
+            for half, (z_codes, z_plane) in enumerate(z_halves):
+                acc = accs.tile([P, HALF], F32, name="acc%d_%d" % (a, half), tag="acc")
+                for side in range(2):
+                    nc.tensor.matmul_mx(
+                        acc[:],
+                        lhsT=codes[:, side * PICK + block * P : side * PICK + (block + 1) * P].bitcast(FP8X4),
+                        lhsT_scale=d_plane[:, side * H + a * P : side * H + (a + 1) * P],
+                        rhs=z_codes[:].bitcast(FP8X4),
+                        rhs_scale=z_plane[:],
+                        start=(side == 0),
+                        stop=(side == 1),
+                    )
+                nc.vector.tensor_scalar(h_blocks[a][:, half * HALF : (half + 1) * HALF], acc[:], 0.0625, None, MULT)
+            return h_blocks[a]
 
         def place_h(a, h):
+            page = keep.tile([P, U], F32, name="page%d" % a)
+            early = HALF if a < PICK // P else 0
+            if early:
+                nc.scalar.activation(page[:].indirect(entries(n1_sb, 0, early)), h[:, 0:early], COPY)
             fetched = keep.tile([P, S], F32, name="fetched%d" % a)
             nc.scalar.activation(fetched[:], h[:].indirect(n3_sb[:]), COPY)
             nw = keep.tile([P, S], F32, name="nw%d" % a)
             nc.vector.tensor_tensor(nw[:], h[:, 0:S], fetched[:], SUBTRACT)
-            page = keep.tile([P, U], F32, name="page%d" % a)
-            nc.scalar.activation(page[:].indirect(n1_sb[:]), h[:, 0:S], COPY)
+            nc.scalar.activation(page[:].indirect(entries(n1_sb, early, S - early)), h[:, early:S], COPY)
             return page, nw
 
         def place_nw(a, page, nw):

from contextlib import ExitStack

import concourse.mybir as mybir

K, T, S, H, G, U = 512, 2048, 256, 512, 2048, 512
FLOPS = 2 * K * H * S + 2 * 2 * K * H * S

F32 = mybir.dt.float32
BF16 = mybir.dt.bfloat16
I32 = mybir.dt.int32
U32 = mybir.dt.uint32
U16 = mybir.dt.uint16
U8 = mybir.dt.uint8
FP8X4 = mybir.dt.float8_e4m3fn_x4
COPY = mybir.ActivationFunctionType.Copy
MULT = mybir.AluOpType.mult
SUBTRACT = mybir.AluOpType.subtract

P = 128
PACK = 4
STRIPE = 16
PICK = 256
HALF = S // 2
SCALAR_SHARE = 64
SPARE = 16
EARLY_ROWS = 2


def entries(offsets, start, count):
    return offsets[:, start // STRIPE : (start + count) // STRIPE]


def tile_picked_hdaqipagq_none_p_kernel(
    tc, x_words, x_scales, w1, gs, d_words, d_scales, offs, ka, kb, n1, n2, n3, out
):
    nc = tc.nc
    with ExitStack() as ctx:
        keep = ctx.enter_context(tc.tile_pool(name="keep", bufs=1))
        psum = ctx.enter_context(tc.psum_pool(name="psum", bufs=1))
        accs = ctx.enter_context(tc.psum_pool(name="accs", bufs=6))

        def load_list(name, source):
            offsets = keep.tile(list(source.shape), U16, name=name)
            nc.sync.dma_start(offsets[:], source)
            return offsets

        def load_scale_table(name, source, zeroing_engine, queue):
            table = keep.tile([P, source.shape[2]], U8, name=name, align_bytes=64)
            zeroing_engine.memset(table[:].bitcast(I32), 0)
            queue.dma_start(table[0:P:8, :].bitcast(I32), source[0].bitcast(I32))
            return table

        def load_word_table(name, source):
            table = keep.tile([P, source.shape[2]], U32, name=name, align_bytes=64)
            nc.sync.dma_start(table[:].bitcast(I32), source[0].rearrange("p n t -> p (n t)").bitcast(I32))
            return table

        def settle_scales(name, picked, width, queues):
            plane = keep.tile([P, width], U8, name=name, align_bytes=64)
            nc.vector.memset(plane[:].bitcast(I32), 0)
            for r in range(4):
                queues[r % len(queues)].dma_start(plane[r:P:32, :].bitcast(I32), picked[8 * r : P : 32, :].bitcast(I32))
            return plane

        gs_sb = keep.tile([P, PACK], F32, name="gs_sb")
        nc.scalar.dma_start(gs_sb[:], gs.rearrange("(p t) o -> p (t o)", t=PACK))
        w_raw = keep.tile([P, PACK, H], F32, name="w_raw")
        w_rows = w1.rearrange("(p j) c -> p j c", j=PACK)
        nc.sync.dma_start(w_raw[:, 0:EARLY_ROWS, :], w_rows[:, 0:EARLY_ROWS, :])
        offs_sb = load_list("offs_sb", offs)
        x_scale_table = load_scale_table("x_scale_table", x_scales, nc.vector, nc.sync)
        ka_sb = load_list("ka_sb", ka)
        d_scale_table = load_scale_table("d_scale_table", d_scales, nc.vector, nc.sync)
        nc.sync.dma_start(w_raw[:, EARLY_ROWS:, :], w_rows[:, EARLY_ROWS:, :])
        x_word_table = load_word_table("x_word_table", x_words)
        kb_sb = load_list("kb_sb", kb)

        h_blocks = [keep.tile([P, S + SPARE], F32, name="h%d" % a) for a in range(H // P)]
        nc.vector.memset(h_blocks[0][:, S:], 0.0)
        for h in h_blocks[1:]:
            nc.scalar.activation(h[:, S:], h_blocks[0][:, S:], COPY)

        x_picked = keep.tile([P, S], U8, name="x_picked", align_bytes=64)
        nc.vector.tensor_copy(x_picked[:], x_scale_table[:].indirect(offs_sb[:]))
        x_plane = settle_scales("x_plane", x_picked, S, (nc.sync,))
        d_word_table = load_word_table("d_word_table", d_words)
        d_picked = keep.tile([P, 2 * H], U8, name="d_picked", tag="d_picked", align_bytes=64)
        nc.vector.tensor_copy(d_picked[:, 0:H], d_scale_table[:].indirect(ka_sb[:]))
        n3_sb = load_list("n3_sb", n3)
        n1_sb = load_list("n1_sb", n1)
        n2_sb = load_list("n2_sb", n2)

        w_bf = keep.tile([P, PACK, P * PACK], BF16, name="w_bf", align_bytes=64)
        w_out = w_bf[:].rearrange("p t (m j) -> p m j t", j=PACK)
        w_in = w_raw[:].rearrange("p j (m t) -> p m j t", t=PACK)
        nc.scalar.activation(w_out[:, 0:SCALAR_SHARE], w_in[:, 0:SCALAR_SHARE], COPY)
        nc.vector.tensor_copy(w_out[:, SCALAR_SHARE:], w_in[:, SCALAR_SHARE:])
        w_codes = keep.tile([P, H], U32, name="w_codes", align_bytes=64)
        w_plane = keep.tile([P, H], U8, name="w_plane", align_bytes=64)
        nc.vector.quantize_mx(w_codes[:].bitcast(FP8X4), w_plane[:], w_bf[:].rearrange("p t c -> p (t c)"))

        x_codes = keep.tile([P, S], U32, name="x_codes", align_bytes=64)
        nc.vector.tensor_copy(x_codes[:], x_word_table[:].indirect(offs_sb[:]))

        nc.vector.tensor_copy(d_picked[:, H:], d_scale_table[:].indirect(kb_sb[:]))
        d_plane = settle_scales("d_plane", d_picked, 2 * H, (nc.sync, nc.scalar))

        def project(half):
            cols = slice(half * HALF, (half + 1) * HALF)
            y = psum.tile([P, PACK, HALF], F32, name="y%d" % half)
            for t in range(PACK):
                rows = slice(t * P, (t + 1) * P)
                nc.tensor.matmul_mx(
                    y[:, t, :],
                    lhsT=w_codes[:, rows].bitcast(FP8X4),
                    lhsT_scale=w_plane[:, rows],
                    rhs=x_codes[:, cols].bitcast(FP8X4),
                    rhs_scale=x_plane[:, cols],
                    start=True,
                    stop=True,
                )
            return y

        def quantise_z(half, z_bf, tag):
            codes = keep.tile([P, HALF], U32, name="z_codes%d" % half, tag=tag, align_bytes=64)
            plane = keep.tile([P, HALF], U8, name="z_plane%d" % half, align_bytes=64)
            nc.vector.quantize_mx(codes[:].bitcast(FP8X4), plane[:], z_bf[:].rearrange("p j t -> p (j t)"))
            return codes, plane

        y_first, y_second = project(0), project(1)
        z_first = keep.tile([P, HALF, PACK], BF16, name="z_first", align_bytes=64)
        nc.vector.tensor_tensor(
            z_first[:],
            y_first[:].rearrange("p t j -> p j t"),
            gs_sb[:].unsqueeze(1).to_broadcast([P, HALF, PACK]),
            MULT,
        )
        z_rows = keep.tile([P, PACK, HALF], BF16, name="z_rows", align_bytes=64)
        for t in range(PACK):
            nc.scalar.activation(z_rows[:, t, :], y_second[:, t, :], COPY, scale=gs_sb[:, t : t + 1])
        z_second = keep.tile([P, HALF, PACK], BF16, name="z_second", align_bytes=64)
        nc.scalar.copy(
            z_second[:].rearrange("p (c i) t -> p c t i", i=PACK),
            z_rows[:].rearrange("p t (c i) -> p c t i", i=PACK),
        )
        z_halves = (quantise_z(0, z_first, "z_codes0"), quantise_z(1, z_second, "d_picked"))

        def pick_words(part):
            codes = keep.tile([P, 2 * PICK], U32, name="d_codes%d" % part, tag="d_codes", align_bytes=64)
            for side, offsets in enumerate((ka_sb, kb_sb)):
                nc.vector.tensor_copy(codes[:, side * PICK : (side + 1) * PICK], d_word_table[:].indirect(entries(offsets, part * PICK, PICK)))
            return codes

        def make_h(a, codes):
            block = a % (PICK // P)
            for half, (z_codes, z_plane) in enumerate(z_halves):
                acc = accs.tile([P, HALF], F32, name="acc%d_%d" % (a, half), tag="acc")
                for side in range(2):
                    nc.tensor.matmul_mx(
                        acc[:],
                        lhsT=codes[:, side * PICK + block * P : side * PICK + (block + 1) * P].bitcast(FP8X4),
                        lhsT_scale=d_plane[:, side * H + a * P : side * H + (a + 1) * P],
                        rhs=z_codes[:].bitcast(FP8X4),
                        rhs_scale=z_plane[:],
                        start=(side == 0),
                        stop=(side == 1),
                    )
                nc.vector.tensor_scalar(h_blocks[a][:, half * HALF : (half + 1) * HALF], acc[:], 0.0625, None, MULT)
            return h_blocks[a]

        def place_h(a, h):
            page = keep.tile([P, U], F32, name="page%d" % a)
            early = HALF if a < PICK // P else 0
            if early:
                nc.scalar.activation(page[:].indirect(entries(n1_sb, 0, early)), h[:, 0:early], COPY)
            fetched = keep.tile([P, S], F32, name="fetched%d" % a)
            nc.scalar.activation(fetched[:], h[:].indirect(n3_sb[:]), COPY)
            nw = keep.tile([P, S], F32, name="nw%d" % a)
            nc.vector.tensor_tensor(nw[:], h[:, 0:S], fetched[:], SUBTRACT)
            nc.scalar.activation(page[:].indirect(entries(n1_sb, early, S - early)), h[:, early:S], COPY)
            return page, nw

        def place_nw(a, page, nw):
            nc.scalar.activation(page[:].indirect(n2_sb[:]), nw[:], COPY)
            nc.sync.dma_start(out[a * P : (a + 1) * P, :], page[:])

        waiting = None
        for a in range(H // P):
            if a % (PICK // P) == 0:
                codes = pick_words(a // (PICK // P))
            placed = place_h(a, make_h(a, codes))
            if waiting is not None:
                place_nw(a - 1, *waiting)
            waiting = placed
        place_nw(H // P - 1, *waiting)
